import numpy as np
import ml_dtypes


def mxq(x, axis, fmt="e4m3"):
    dtype, down = {"e4m3": (ml_dtypes.float8_e4m3fn, 7), "e5m2": (ml_dtypes.float8_e5m2, 14)}[fmt]
    v = np.moveaxis(np.asarray(x, np.float32).astype(ml_dtypes.bfloat16).astype(np.float64), axis, -1)
    blocks = v.reshape(v.shape[:-1] + (-1, 32))
    amax = np.abs(blocks).max(-1, keepdims=True)
    byte = np.maximum(np.where(amax > 0, np.frexp(amax)[1] - 1 + 127, 0) - down, 1)
    scale = np.exp2(byte - 127.0)
    codes = (blocks / scale).astype(np.float32).astype(dtype).astype(np.float64)
    return np.moveaxis((codes * scale).reshape(v.shape), -1, axis)


WIDE = False


def mx_kscale(k):
    if not WIDE:
        return np.ones(k)
    levels = np.array([10, -10, 5, -5, 0])
    if k % 512:
        return np.exp2(np.random.permutation(np.resize(levels, k // 32))).repeat(32)
    a = np.empty((k // 512, 16))
    for p in range(k // 512):
        a[p, :8] = np.random.permutation(np.resize(levels, 8))
        for g in range(8):
            far = levels[np.abs(levels - a[p, g]) >= 10]
            a[p, g + 8] = far[np.random.randint(len(far))]
    return np.exp2(a.ravel()).repeat(32)


def f64(x):
    return np.asarray(x).astype(np.float64)


def striped(idx):
    return np.tile(idx.reshape(-1, 16).T, (8, 1)).astype(np.uint16)


def unstriped(offs):
    return offs[:16].T.reshape(-1).astype(np.int64)


E2M1 = np.array([0.0, 0.5, 1.0, 1.5, 2.0, 3.0, 4.0, 6.0, -0.0, -0.5, -1.0, -1.5, -2.0, -3.0, -4.0, -6.0])


def pack_weight(w, fmt):
    k, n = w.shape
    w = f64(np.asarray(w, np.float32).astype(ml_dtypes.bfloat16)).reshape(k // 32, 32, n)
    amax = np.abs(w).max(1)
    if fmt == "e4m3":
        byte = np.frexp(amax)[1] - 1 + 127 - 7
    else:
        mant, ex = np.frexp(amax / 6.0)
        byte = np.where(mant > 0.5, ex, ex - 1) + 127
    byte = np.clip(np.where(amax > 0, byte, 1), 1, 254)
    scaled = (w * np.exp2(127.0 - byte)[:, None, :]).reshape(k, n).astype(np.float32)
    by_word = np.ascontiguousarray(scaled.reshape(k // 512, 128, 4, n).transpose(0, 1, 3, 2))
    if fmt == "e4m3":
        words = by_word.astype(ml_dtypes.float8_e4m3fn).view(np.uint8)
    else:
        c = by_word.astype(ml_dtypes.float4_e2m1fn).view(np.uint8) & 0xF
        words = (c[..., 0::2] | (c[..., 1::2] << 4)).reshape(k // 512, 128, 2 * n)
    return np.ascontiguousarray(words), np.ascontiguousarray(byte.astype(np.uint8).reshape(k // 512, 16, n))


def unpack_weight(words, scales, fmt):
    g, _, n = scales.shape
    words = np.ascontiguousarray(words).reshape(g, 128, n, -1)
    if fmt == "e4m3":
        vals = words.view(ml_dtypes.float8_e4m3fn).astype(np.float64)
    else:
        nib = np.empty((g, 128, n, 4), np.uint8)
        nib[..., 0::2] = words & 0xF
        nib[..., 1::2] = words >> 4
        vals = E2M1[nib]
    vals = vals * np.repeat(np.exp2(scales.astype(np.float64) - 127.0), 8, axis=1)[..., None]
    return vals.transpose(0, 1, 3, 2).reshape(g * 512, n)


def gelu(v):
    return 0.5 * v * (1.0 + np.tanh(np.sqrt(2.0 / np.pi) * (v + 0.044715 * v**3)))


K, H, N, T, S, P = 1536, 1024, 768, 4096, 1024, 512

def setup_inputs():
    n = np.random.standard_normal
    s = mx_kscale(K)[:, None]
    u = mx_kscale(H)[:, None]
    tab_words, tab_scales = pack_weight(n((K, T)) * s, "e4m3")
    w4_words, w4_scales = pack_weight(2.0 * n((H, N)) / np.sqrt(H) / u, "e2m1")
    return {
        "tab_words": tab_words, "tab_scales": tab_scales,
        "offs": striped(np.random.permutation(T)[:S]),
        "pos1": striped(np.random.permutation(S)[:P]),
        "pos2": striped(np.random.permutation(S)[:P]),
        "w1": (0.72 * n((K, H)) / np.sqrt(K) / s).astype(np.float32),
        "gain": (np.random.uniform(1.0, 5.0, H) * u[:, 0]).astype(np.float32),
        "w4_words": w4_words, "w4_scales": w4_scales,
        "last_round": (0.6 * n((N, P))).astype(np.float32),
    }

def reference(tab_words, tab_scales, offs, pos1, pos2, w1, gain, w4_words, w4_scales, last_round):
    v = unpack_weight(tab_words, tab_scales, "e4m3")[:, unstriped(offs)]
    w4 = unpack_weight(w4_words, w4_scales, "e2m1")
    h = mxq(f64(w1), 0, "e4m3").T @ v
    top = h.max(axis=1)
    a = np.exp(h[:, unstriped(pos1)] - top[:, None])
    c = h[:, unstriped(pos2)]
    e = a * c * f64(gain)[:, None]
    eq = mxq(e, 0, "e4m3")
    out = (w4.T @ eq) + f64(last_round)
    return out

@@ -1,0 +1,288 @@
+from contextlib import ExitStack
+
+import concourse.mybir as mybir
+
+K, H, N, T, S, M = 1536, 1024, 768, 4096, 1024, 512
+FLOPS = 2 * K * H * S + 2 * H * N * M
+
+F32 = mybir.dt.float32
+BF16 = mybir.dt.bfloat16
+I32 = mybir.dt.int32
+U32 = mybir.dt.uint32
+U16 = mybir.dt.uint16
+U8 = mybir.dt.uint8
+FP8X4 = mybir.dt.float8_e4m3fn_x4
+FP4X4 = mybir.dt.float4_e2m1fn_x4
+ALU = mybir.AluOpType
+ACT = mybir.ActivationFunctionType
+
+P = 128
+PACK = 4
+PASS = P * PACK
+KP = K // PASS
+HP = H // PASS
+BANK = 512
+HALF = M // 2
+
+
+def tile_list_ward_alarm_board_kernel(
+    tc, tab_words, tab_scales, offs, pos1, pos2, w1, gain, w4_words, w4_scales, last_round, out
+):
+    nc = tc.nc
+    with ExitStack() as ctx:
+        lists = ctx.enter_context(tc.tile_pool(name="lists", bufs=1))
+        keep = ctx.enter_context(tc.tile_pool(name="keep", bufs=1))
+        ring = ctx.enter_context(tc.tile_pool(name="ring", bufs=3))
+        psum = ctx.enter_context(tc.psum_pool(name="psum", bufs=1))
+
+        idx = lists.tile([P, S // 16], U16, name="idx")
+        p1 = lists.tile([P, M // 16], U16, name="p1")
+        p2 = lists.tile([P, M // 16], U16, name="p2")
+
+        tab = [keep.tile([P, T], I32, name="tab%d" % a, align_bytes=64) for a in range(KP)]
+        tab_s = keep.tile([P, T], U8, name="tab_s", align_bytes=64)
+        v = [keep.tile([P, S], U32, name="v%d" % a, align_bytes=64) for a in range(KP)]
+        v_s = keep.tile([P, S], U8, name="v_s", align_bytes=64)
+        raw = {(b, a): keep.tile([P, PACK, PASS], F32, name="raw%d%d" % (b, a)) for b in range(HP) for a in range(KP)}
+        wq = {(b, a): keep.tile([P, PASS], U32, name="wq%d%d" % (b, a), align_bytes=64) for b in range(HP) for a in range(KP)}
+        wq_s = {(b, a): keep.tile([P, PASS], U8, name="wqs%d%d" % (b, a), align_bytes=64) for b in range(HP) for a in range(KP)}
+        gains = keep.tile([P, HP, PACK], F32, name="gains")
+        w4 = keep.tile([P, HP, 2 * N], U8, name="w4", align_bytes=64)
+        w4_s = keep.tile([P, HP, N], U8, name="w4_s", align_bytes=64)
+        res = [keep.tile([P, 2, M], F32, name="res%d" % i) for i in range(N // (2 * P))]
+        h = {(b, t): keep.tile([P, S], F32, name="h%d%d" % (b, t)) for b in range(HP) for t in range(PACK)}
+        tops = {(b, t): keep.tile([P, 2], F32, name="tops%d%d" % (b, t)) for b in range(HP) for t in range(PACK)}
+        neg = {(b, t): keep.tile([P, 1], F32, name="neg%d%d" % (b, t)) for b in range(HP) for t in range(PACK)}
+        e_rows = [keep.tile([P, PACK, M], BF16, name="e_rows0"), keep.tile([P, PACK, M], BF16, name="e_rows1")]
+        e_grp = [keep.tile([P, M, PACK], BF16, name="e_grp%d" % b, align_bytes=64) for b in range(HP)]
+        eq = [keep.tile([P, M], U32, name="eq%d" % b, align_bytes=64) for b in range(HP)]
+        eq_s = [keep.tile([P, M], U8, name="eq_s%d" % b, align_bytes=64) for b in range(HP)]
+
+        def load_tab(a):
+            nc.sync.dma_start(out=tab[a][:], in_=tab_words[a].rearrange("p n t -> p (n t)").bitcast(I32))
+
+        def load_w1(b, a):
+            rows = w1[a * PASS : (a + 1) * PASS, b * PASS : (b + 1) * PASS]
+            nc.sync.dma_start(out=raw[b, a][:], in_=rows.rearrange("(p j) c -> p j c", j=PACK))
+
+        nc.vector.memset(tab_s[:].bitcast(I32), 0)
+        nc.vector.memset(w4_s[:].bitcast(I32), 0)
+        load_tab(0)
+        for q in range(4):
+            nc.sync.dma_start(
+                out=tab_s[32 * q : 32 * q + 4 * KP, :].bitcast(I32),
+                in_=tab_scales[:, 4 * q : 4 * q + 4, :].bitcast(I32),
+            )
+        nc.sync.dma_start(idx[:], offs)
+        for a in range(KP):
+            if a > 0:
+                load_tab(a)
+            load_w1(0, a)
+        nc.sync.dma_start(out=gains[:], in_=gain.rearrange("(b p t) -> p b t", b=HP, t=PACK))
+        nc.sync.dma_start(p1[:], pos1)
+        nc.sync.dma_start(p2[:], pos2)
+        for a in range(KP):
+            load_w1(1, a)
+        nc.sync.dma_start(out=w4[:].bitcast(I32), in_=w4_words.rearrange("a p c -> p a c").bitcast(I32))
+        for q in range(4):
+            nc.gpsimd.dma_start(
+                out=w4_s[32 * q : 32 * q + 4, :, :].bitcast(I32),
+                in_=w4_scales[:, 4 * q : 4 * q + 4, :].rearrange("a r n -> r a n").bitcast(I32),
+            )
+        for i in range(len(res)):
+            rows = last_round[2 * P * i : 2 * P * (i + 1), :]
+            nc.sync.dma_start(out=res[i][:], in_=rows.rearrange("(u p) m -> p u m", p=P))
+
+        def gather_tab(a):
+            nc.vector.tensor_copy(v[a][:], tab[a][:].bitcast(U32).indirect(idx[:]))
+
+        grouped = {}
+
+        def cast_w1(b, a, vector_share):
+            g = ring.tile([P, PACK, P, PACK], BF16, name="grouped", align_bytes=64)
+            grouped[b, a] = g
+            src = raw[b, a][:].rearrange("p j (m t) -> p m t j", t=PACK)
+            dst = g[:].rearrange("p t m j -> p m t j")
+            if vector_share > 0:
+                nc.vector.tensor_copy(out=dst[:, :vector_share], in_=src[:, :vector_share])
+            if vector_share < P:
+                nc.scalar.copy(out=dst[:, vector_share:], in_=src[:, vector_share:])
+
+        def quant_w1(b, a, pieces):
+            g = grouped[b, a][:].rearrange("p t m j -> p (t m j)")
+            w = PASS // pieces
+            for s in range(pieces):
+                nc.vector.quantize_mx(
+                    out=wq[b, a][:, s * w : (s + 1) * w].bitcast(FP8X4),
+                    scales=wq_s[b, a][:, s * w : (s + 1) * w],
+                    in_=g[:, s * w * PACK : (s + 1) * w * PACK],
+                )
+
+        banks = {}
+
+        def first_product(b, a):
+            for t in range(PACK):
+                for c in range(S // BANK):
+                    if a == 0:
+                        banks[b, t, c] = psum.tile([P, BANK], F32, name="bank%d" % (2 * t + c))
+                    cols = slice(c * BANK, (c + 1) * BANK)
+                    nc.tensor.matmul_mx(
+                        out=banks[b, t, c][:],
+                        lhsT=wq[b, a][:, t * P : (t + 1) * P].bitcast(FP8X4),
+                        lhsT_scale=wq_s[b, a][:, t * P : (t + 1) * P],
+                        rhs=v[a][:, cols].bitcast(FP8X4),
+                        rhs_scale=v_s[4 * a : P, cols],
+                        start=(a == 0),
+                        stop=(a == KP - 1),
+                    )
+
+        def evacuate(b, t):
+            for c in range(S // BANK):
+                nc.vector.tensor_scalar(
+                    out=h[b, t][:, c * BANK : (c + 1) * BANK],
+                    in0=banks[b, t, c][:],
+                    scalar1=1.0,
+                    scalar2=None,
+                    op0=ALU.mult,
+                    op1=ALU.max,
+                    accum_out=tops[b, t][:, c : c + 1],
+                )
+            nc.gpsimd.tensor_scalar(
+                out=neg[b, t][:], in0=tops[b, t][:, 0:1], scalar1=tops[b, t][:, 1:2], scalar2=-1.0, op0=ALU.max, op1=ALU.mult
+            )
+
+        looks = {}
+        picks = {}
+
+        def look(b, t, lo, n):
+            a_t = ring.tile([P, n], F32, name="look%d" % n, bufs=4)
+            looks[b, t, lo] = a_t
+            nc.scalar.activation(
+                out=a_t[:], in_=h[b, t][:].indirect(p1[:, lo // 16 : (lo + n) // 16]), func=ACT.Exp, bias=neg[b, t][:]
+            )
+
+        def pick(b, t, lo, n):
+            c_t = ring.tile([P, n], F32, name="pick%d" % n, bufs=4)
+            picks[b, t, lo] = c_t
+            nc.vector.tensor_copy(c_t[:], h[b, t][:].indirect(p2[:, lo // 16 : (lo + n) // 16]))
+
+        def product(b, t, lo, n):
+            nc.vector.scalar_tensor_tensor(
+                out=e_rows[b][:, t, lo : lo + n],
+                in0=picks[b, t, lo][:],
+                scalar=gains[:, b, t : t + 1],
+                in1=looks[b, t, lo][:],
+                op0=ALU.mult,
+                op1=ALU.mult,
+            )
+
+        def scale_look(b, t, lo, n):
+            c_t = ring.tile([P, n], F32, name="pick%d" % n, bufs=4)
+            picks[b, t, lo] = c_t
+            nc.scalar.activation(out=c_t[:], in_=looks[b, t, lo][:], func=ACT.Copy, scale=gains[:, b, t : t + 1])
+
+        def fused(b, t, lo, n):
+            nc.vector.tensor_tensor(
+                e_rows[b][:, t, lo : lo + n],
+                h[b, t][:].indirect(p2[:, lo // 16 : (lo + n) // 16]),
+                picks[b, t, lo][:],
+                ALU.mult,
+            )
+
+        def group_e(b, lo, n):
+            src = e_rows[b][:, :, lo : lo + n].rearrange("p t (c i) -> p c t i", i=4)
+            dst = e_grp[b][:, lo : lo + n, :].rearrange("p (c i) t -> p c t i", i=4)
+            nc.scalar.copy(out=dst, in_=src)
+
+        def quant_e(b, lo, n):
+            nc.vector.quantize_mx(
+                out=eq[b][:, lo : lo + n].bitcast(FP8X4),
+                scales=eq_s[b][:, lo : lo + n],
+                in_=e_grp[b][:, lo : lo + n, :].rearrange("p m t -> p (m t)"),
+            )
+
+        acc = {}
+
+        def second_product(b, half):
+            cols = slice(half * HALF, (half + 1) * HALF)
+            for i in range(len(res)):
+                if b == 0:
+                    acc[i, half] = psum.tile([P, 2, HALF], F32, name="bank%d" % (len(res) * half + i))
+                for u in range(2):
+                    n0 = (2 * i + u) * P
+                    nc.tensor.matmul_mx(
+                        out=acc[i, half][:, u, :],
+                        lhsT=w4[:, b, 2 * n0 : 2 * (n0 + P)].bitcast(FP4X4),
+                        lhsT_scale=w4_s[:, b, n0 : n0 + P],
+                        rhs=eq[b][:, cols].bitcast(FP8X4),
+                        rhs_scale=eq_s[b][:, cols],
+                        start=(b == 0 and u == 0),
+                        stop=(b == HP - 1 and u == 1),
+                    )
+
+        def finish(half):
+            cols = slice(half * HALF, (half + 1) * HALF)
+            for i in range(len(res)):
+                nc.vector.tensor_tensor(res[i][:, :, cols], acc[i, half][:], res[i][:, :, cols], ALU.add)
+                rows = out[2 * P * i : 2 * P * (i + 1), cols]
+                nc.sync.dma_start(out=rows.rearrange("(u p) m -> p u m", p=P), in_=res[i][:, :, cols])
+
+        nc.vector.tensor_copy(v_s[:], tab_s[:].indirect(idx[:]))
+        for a in range(KP):
+            gather_tab(a)
+            last = a == KP - 1
+            cast_w1(0, a, 80 if last else 0)
+            quant_w1(0, a, 4 if last else 1)
+            first_product(0, a)
+
+        evacuate(0, 0)
+        look(0, 0, 0, M)
+        cast_w1(1, 0, 0)
+        for t in range(PACK):
+            if t + 1 < PACK:
+                evacuate(0, t + 1)
+                look(0, t + 1, 0, M)
+            pick(0, t, 0, M)
+            if t > 0:
+                product(0, t - 1, 0, M)
+            if t == 1:
+                quant_w1(1, 0, 1)
+                first_product(1, 0)
+                cast_w1(1, 1, 0)
+        cast_w1(1, 2, 0)
+        quant_w1(1, 1, 1)
+        first_product(1, 1)
+        product(0, PACK - 1, 0, M)
+        quant_w1(1, 2, 4)
+        first_product(1, 2)
+        group_e(0, 0, M)
+
+        evacuate(1, 0)
+        look(1, 0, 0, HALF)
+        for t in range(PACK):
+            if t + 1 < PACK:
+                evacuate(1, t + 1)
+                look(1, t + 1, 0, HALF)
+            pick(1, t, 0, HALF)
+            if t > 0:
+                product(1, t - 1, 0, HALF)
+            if t == 1:
+                quant_e(0, 0, M)
+        second_product(0, 0)
+        second_product(0, 1)
+        for t in range(PACK):
+            look(1, t, HALF, HALF)
+        pick(1, 0, HALF, HALF)
+        product(1, PACK - 1, 0, HALF)
+        group_e(1, 0, HALF)
+        for t in range(PACK):
+            if t + 1 < PACK:
+                pick(1, t + 1, HALF, HALF)
+            product(1, t, HALF, HALF)
+        group_e(1, HALF, HALF)
+        quant_e(1, 0, HALF)
+        second_product(1, 0)
+        finish(0)
+        quant_e(1, HALF, HALF)
+        second_product(1, 1)
+        finish(1)

@@ -19,270 +19,212 @@ ACT = mybir.ActivationFunctionType
 P = 128
 PACK = 4
 PASS = P * PACK
-KP = K // PASS
-HP = H // PASS
+K_PASSES = K // PASS
+R_PASSES = H // PASS
+QUADRANTS = 4
 BANK = 512
 HALF = M // 2
+N_PAIRS = N // (2 * P)
+PER_COLUMN = 16
 
 
 def tile_list_ward_alarm_board_kernel(
     tc, tab_words, tab_scales, offs, pos1, pos2, w1, gain, w4_words, w4_scales, last_round, out
 ):
     nc = tc.nc
+    w1_chunks = [(b, a) for b in range(R_PASSES) for a in range(K_PASSES)]
+    row_sets = [(b, t) for b in range(R_PASSES) for t in range(PACK)]
+
     with ExitStack() as ctx:
         lists = ctx.enter_context(tc.tile_pool(name="lists", bufs=1))
         keep = ctx.enter_context(tc.tile_pool(name="keep", bufs=1))
-        ring = ctx.enter_context(tc.tile_pool(name="ring", bufs=3))
+        stage = ctx.enter_context(tc.tile_pool(name="stage", bufs=K_PASSES))
         psum = ctx.enter_context(tc.psum_pool(name="psum", bufs=1))
 
-        idx = lists.tile([P, S // 16], U16, name="idx")
-        p1 = lists.tile([P, M // 16], U16, name="p1")
-        p2 = lists.tile([P, M // 16], U16, name="p2")
+        idx = lists.tile([P, S // PER_COLUMN], U16, name="idx")
+        p1 = lists.tile([P, M // PER_COLUMN], U16, name="p1")
+        p2 = lists.tile([P, M // PER_COLUMN], U16, name="p2")
 
-        tab = [keep.tile([P, T], I32, name="tab%d" % a, align_bytes=64) for a in range(KP)]
+        tab = [keep.tile([P, T], I32, name="tab%d" % a, align_bytes=64) for a in range(K_PASSES)]
         tab_s = keep.tile([P, T], U8, name="tab_s", align_bytes=64)
-        v = [keep.tile([P, S], U32, name="v%d" % a, align_bytes=64) for a in range(KP)]
+        v = [keep.tile([P, S], U32, name="v%d" % a, align_bytes=64) for a in range(K_PASSES)]
         v_s = keep.tile([P, S], U8, name="v_s", align_bytes=64)
-        raw = {(b, a): keep.tile([P, PACK, PASS], F32, name="raw%d%d" % (b, a)) for b in range(HP) for a in range(KP)}
-        wq = {(b, a): keep.tile([P, PASS], U32, name="wq%d%d" % (b, a), align_bytes=64) for b in range(HP) for a in range(KP)}
-        wq_s = {(b, a): keep.tile([P, PASS], U8, name="wqs%d%d" % (b, a), align_bytes=64) for b in range(HP) for a in range(KP)}
-        gains = keep.tile([P, HP, PACK], F32, name="gains")
-        w4 = keep.tile([P, HP, 2 * N], U8, name="w4", align_bytes=64)
-        w4_s = keep.tile([P, HP, N], U8, name="w4_s", align_bytes=64)
-        res = [keep.tile([P, 2, M], F32, name="res%d" % i) for i in range(N // (2 * P))]
-        h = {(b, t): keep.tile([P, S], F32, name="h%d%d" % (b, t)) for b in range(HP) for t in range(PACK)}
-        tops = {(b, t): keep.tile([P, 2], F32, name="tops%d%d" % (b, t)) for b in range(HP) for t in range(PACK)}
-        neg = {(b, t): keep.tile([P, 1], F32, name="neg%d%d" % (b, t)) for b in range(HP) for t in range(PACK)}
-        e_rows = [keep.tile([P, PACK, M], BF16, name="e_rows0"), keep.tile([P, PACK, M], BF16, name="e_rows1")]
-        e_grp = [keep.tile([P, M, PACK], BF16, name="e_grp%d" % b, align_bytes=64) for b in range(HP)]
-        eq = [keep.tile([P, M], U32, name="eq%d" % b, align_bytes=64) for b in range(HP)]
-        eq_s = [keep.tile([P, M], U8, name="eq_s%d" % b, align_bytes=64) for b in range(HP)]
+        w1_raw = {c: keep.tile([P, PACK, PASS], F32, name="w1_raw%d%d" % c) for c in w1_chunks}
+        w1_q = {c: keep.tile([P, PASS], U32, name="w1_q%d%d" % c, align_bytes=64) for c in w1_chunks}
+        w1_s = {c: keep.tile([P, PASS], U8, name="w1_s%d%d" % c, align_bytes=64) for c in w1_chunks}
+        gains = keep.tile([P, R_PASSES, PACK], F32, name="gains")
+        w4 = keep.tile([P, R_PASSES, 2 * N], U8, name="w4", align_bytes=64)
+        w4_s = keep.tile([P, R_PASSES, N], U8, name="w4_s", align_bytes=64)
+        result = [keep.tile([P, 2, M], F32, name="result%d" % i) for i in range(N_PAIRS)]
+        h = {r: keep.tile([P, S], F32, name="h%d%d" % r) for r in row_sets}
+        bank_tops = {r: keep.tile([P, S // BANK], F32, name="bank_tops%d%d" % r) for r in row_sets}
+        neg_top = {r: keep.tile([P, 1], F32, name="neg_top%d%d" % r) for r in row_sets}
+        looked = {r: keep.tile([P, M], F32, name="looked%d%d" % r) for r in row_sets}
+        e_rows = [keep.tile([P, PACK, M], F32, name="e_rows%d" % b) for b in range(R_PASSES)]
+        e_words = [keep.tile([P, M, PACK], BF16, name="e_words%d" % b, align_bytes=64) for b in range(R_PASSES)]
+        e_q = [keep.tile([P, M], U32, name="e_q%d" % b, align_bytes=64) for b in range(R_PASSES)]
+        e_s = [keep.tile([P, M], U8, name="e_s%d" % b, align_bytes=64) for b in range(R_PASSES)]
 
-        def load_tab(a):
-            nc.sync.dma_start(out=tab[a][:], in_=tab_words[a].rearrange("p n t -> p (n t)").bitcast(I32))
+        def load_table(a):
+            nc.sync.dma_start(out=tab[a][:], in_=tab_words[a].rearrange("p n i -> p (n i)").bitcast(I32))
 
         def load_w1(b, a):
             rows = w1[a * PASS : (a + 1) * PASS, b * PASS : (b + 1) * PASS]
-            nc.sync.dma_start(out=raw[b, a][:], in_=rows.rearrange("(p j) c -> p j c", j=PACK))
+            nc.sync.dma_start(out=w1_raw[b, a][:], in_=rows.rearrange("(p j) c -> p j c", j=PACK))
 
         nc.vector.memset(tab_s[:].bitcast(I32), 0)
         nc.vector.memset(w4_s[:].bitcast(I32), 0)
-        load_tab(0)
-        for q in range(4):
+        load_table(0)
+        for q in range(QUADRANTS):
             nc.sync.dma_start(
-                out=tab_s[32 * q : 32 * q + 4 * KP, :].bitcast(I32),
+                out=tab_s[32 * q : 32 * q + 4 * K_PASSES, :].bitcast(I32),
                 in_=tab_scales[:, 4 * q : 4 * q + 4, :].bitcast(I32),
             )
         nc.sync.dma_start(idx[:], offs)
-        for a in range(KP):
-            if a > 0:
-                load_tab(a)
+        load_w1(0, 0)
+        for a in range(1, K_PASSES):
+            load_table(a)
             load_w1(0, a)
-        nc.sync.dma_start(out=gains[:], in_=gain.rearrange("(b p t) -> p b t", b=HP, t=PACK))
+        nc.sync.dma_start(out=gains[:], in_=gain.rearrange("(b p t) -> p b t", b=R_PASSES, t=PACK))
         nc.sync.dma_start(p1[:], pos1)
         nc.sync.dma_start(p2[:], pos2)
-        for a in range(KP):
+        for a in range(K_PASSES):
             load_w1(1, a)
-        nc.sync.dma_start(out=w4[:].bitcast(I32), in_=w4_words.rearrange("a p c -> p a c").bitcast(I32))
-        for q in range(4):
-            nc.gpsimd.dma_start(
+        nc.sync.dma_start(out=w4[:].bitcast(I32), in_=w4_words.rearrange("b p c -> p b c").bitcast(I32))
+        for q in range(QUADRANTS):
+            nc.sync.dma_start(
                 out=w4_s[32 * q : 32 * q + 4, :, :].bitcast(I32),
-                in_=w4_scales[:, 4 * q : 4 * q + 4, :].rearrange("a r n -> r a n").bitcast(I32),
+                in_=w4_scales[:, 4 * q : 4 * q + 4, :].rearrange("b r n -> r b n").bitcast(I32),
             )
-        for i in range(len(res)):
+        for i in range(N_PAIRS):
             rows = last_round[2 * P * i : 2 * P * (i + 1), :]
-            nc.sync.dma_start(out=res[i][:], in_=rows.rearrange("(u p) m -> p u m", p=P))
+            nc.sync.dma_start(out=result[i][:], in_=rows.rearrange("(u p) m -> p u m", p=P))
 
-        def gather_tab(a):
-            nc.vector.tensor_copy(v[a][:], tab[a][:].bitcast(U32).indirect(idx[:]))
-
-        grouped = {}
-
-        def cast_w1(b, a, vector_share):
-            g = ring.tile([P, PACK, P, PACK], BF16, name="grouped", align_bytes=64)
-            grouped[b, a] = g
-            src = raw[b, a][:].rearrange("p j (m t) -> p m t j", t=PACK)
-            dst = g[:].rearrange("p t m j -> p m t j")
-            if vector_share > 0:
-                nc.vector.tensor_copy(out=dst[:, :vector_share], in_=src[:, :vector_share])
-            if vector_share < P:
-                nc.scalar.copy(out=dst[:, vector_share:], in_=src[:, vector_share:])
-
-        def quant_w1(b, a, pieces):
-            g = grouped[b, a][:].rearrange("p t m j -> p (t m j)")
-            w = PASS // pieces
-            for s in range(pieces):
+        def quantise_w1(b, a, first_copy, pieces):
+            rounded = stage.tile([P, PACK, P, PACK], BF16, name="rounded", align_bytes=64)
+            src = w1_raw[b, a][:].rearrange("p j (m u s) -> p u m j s", u=2, s=2)
+            dst = rounded[:].rearrange("p (u s) m j -> p u m j s", u=2)
+            first_copy(out=dst[:, 0], in_=src[:, 0])
+            nc.scalar.copy(out=dst[:, 1], in_=src[:, 1])
+            flat = rounded[:].rearrange("p t m j -> p (t m j)")
+            width = PASS // pieces
+            for lo in range(0, PASS, width):
                 nc.vector.quantize_mx(
-                    out=wq[b, a][:, s * w : (s + 1) * w].bitcast(FP8X4),
-                    scales=wq_s[b, a][:, s * w : (s + 1) * w],
-                    in_=g[:, s * w * PACK : (s + 1) * w * PACK],
+                    out=w1_q[b, a][:, lo : lo + width].bitcast(FP8X4),
+                    scales=w1_s[b, a][:, lo : lo + width],
+                    in_=flat[:, lo * PACK : (lo + width) * PACK],
                 )
 
-        banks = {}
+        h_banks = {}
 
-        def first_product(b, a):
-            for t in range(PACK):
-                for c in range(S // BANK):
-                    if a == 0:
-                        banks[b, t, c] = psum.tile([P, BANK], F32, name="bank%d" % (2 * t + c))
-                    cols = slice(c * BANK, (c + 1) * BANK)
-                    nc.tensor.matmul_mx(
-                        out=banks[b, t, c][:],
-                        lhsT=wq[b, a][:, t * P : (t + 1) * P].bitcast(FP8X4),
-                        lhsT_scale=wq_s[b, a][:, t * P : (t + 1) * P],
-                        rhs=v[a][:, cols].bitcast(FP8X4),
-                        rhs_scale=v_s[4 * a : P, cols],
-                        start=(a == 0),
-                        stop=(a == KP - 1),
-                    )
+        def first_product(b, t, a):
+            for c in range(S // BANK):
+                if a == 0:
+                    h_banks[b, t, c] = psum.tile([P, BANK], F32, name="bank%d" % (t * (S // BANK) + c))
+                cols = slice(c * BANK, (c + 1) * BANK)
+                nc.tensor.matmul_mx(
+                    out=h_banks[b, t, c][:],
+                    lhsT=w1_q[b, a][:, t * P : (t + 1) * P].bitcast(FP8X4),
+                    lhsT_scale=w1_s[b, a][:, t * P : (t + 1) * P],
+                    rhs=v[a][:, cols].bitcast(FP8X4),
+                    rhs_scale=v_s[4 * a : P, cols],
+                    start=(a == 0),
+                    stop=(a == K_PASSES - 1),
+                )
 
         def evacuate(b, t):
             for c in range(S // BANK):
                 nc.vector.tensor_scalar(
                     out=h[b, t][:, c * BANK : (c + 1) * BANK],
-                    in0=banks[b, t, c][:],
+                    in0=h_banks[b, t, c][:],
                     scalar1=1.0,
                     scalar2=None,
                     op0=ALU.mult,
                     op1=ALU.max,
-                    accum_out=tops[b, t][:, c : c + 1],
+                    accum_out=bank_tops[b, t][:, c : c + 1],
                 )
             nc.gpsimd.tensor_scalar(
-                out=neg[b, t][:], in0=tops[b, t][:, 0:1], scalar1=tops[b, t][:, 1:2], scalar2=-1.0, op0=ALU.max, op1=ALU.mult
-            )
-
-        looks = {}
-        picks = {}
-
-        def look(b, t, lo, n):
-            a_t = ring.tile([P, n], F32, name="look%d" % n, bufs=4)
-            looks[b, t, lo] = a_t
-            nc.scalar.activation(
-                out=a_t[:], in_=h[b, t][:].indirect(p1[:, lo // 16 : (lo + n) // 16]), func=ACT.Exp, bias=neg[b, t][:]
-            )
-
-        def pick(b, t, lo, n):
-            c_t = ring.tile([P, n], F32, name="pick%d" % n, bufs=4)
-            picks[b, t, lo] = c_t
-            nc.vector.tensor_copy(c_t[:], h[b, t][:].indirect(p2[:, lo // 16 : (lo + n) // 16]))
-
-        def product(b, t, lo, n):
-            nc.vector.scalar_tensor_tensor(
-                out=e_rows[b][:, t, lo : lo + n],
-                in0=picks[b, t, lo][:],
-                scalar=gains[:, b, t : t + 1],
-                in1=looks[b, t, lo][:],
-                op0=ALU.mult,
+                out=neg_top[b, t][:],
+                in0=bank_tops[b, t][:, 0:1],
+                scalar1=bank_tops[b, t][:, 1:2],
+                scalar2=-1.0,
+                op0=ALU.max,
                 op1=ALU.mult,
             )
 
-        def scale_look(b, t, lo, n):
-            c_t = ring.tile([P, n], F32, name="pick%d" % n, bufs=4)
-            picks[b, t, lo] = c_t
-            nc.scalar.activation(out=c_t[:], in_=looks[b, t, lo][:], func=ACT.Copy, scale=gains[:, b, t : t + 1])
+        def make_e(b, t, lo, n):
+            cols = slice(lo, lo + n)
+            entries = slice(lo // PER_COLUMN, (lo + n) // PER_COLUMN)
+            look = looked[b, t][:, cols]
+            nc.scalar.activation(out=look, in_=h[b, t][:].indirect(p1[:, entries]), func=ACT.Exp, bias=neg_top[b, t][:])
+            nc.scalar.activation(out=look, in_=look, func=ACT.Copy, scale=gains[:, b, t : t + 1])
+            nc.vector.tensor_tensor(e_rows[b][:, t, cols], h[b, t][:].indirect(p2[:, entries]), look, ALU.mult)
 
-        def fused(b, t, lo, n):
-            nc.vector.tensor_tensor(
-                e_rows[b][:, t, lo : lo + n],
-                h[b, t][:].indirect(p2[:, lo // 16 : (lo + n) // 16]),
-                picks[b, t, lo][:],
-                ALU.mult,
+        def quantise_e(b, half):
+            cols = slice(half * HALF, (half + 1) * HALF)
+            nc.scalar.copy(
+                out=e_words[b][:, cols, :].rearrange("p (c i) t -> p c t i", i=4),
+                in_=e_rows[b][:, :, cols].rearrange("p t (c i) -> p c t i", i=4),
             )
-
-        def group_e(b, lo, n):
-            src = e_rows[b][:, :, lo : lo + n].rearrange("p t (c i) -> p c t i", i=4)
-            dst = e_grp[b][:, lo : lo + n, :].rearrange("p (c i) t -> p c t i", i=4)
-            nc.scalar.copy(out=dst, in_=src)
-
-        def quant_e(b, lo, n):
             nc.vector.quantize_mx(
-                out=eq[b][:, lo : lo + n].bitcast(FP8X4),
-                scales=eq_s[b][:, lo : lo + n],
-                in_=e_grp[b][:, lo : lo + n, :].rearrange("p m t -> p (m t)"),
+                out=e_q[b][:, cols].bitcast(FP8X4),
+                scales=e_s[b][:, cols],
+                in_=e_words[b][:, cols, :].rearrange("p m t -> p (m t)"),
             )
 
-        acc = {}
+        out_banks = {}
 
         def second_product(b, half):
             cols = slice(half * HALF, (half + 1) * HALF)
-            for i in range(len(res)):
+            for i in range(N_PAIRS):
                 if b == 0:
-                    acc[i, half] = psum.tile([P, 2, HALF], F32, name="bank%d" % (len(res) * half + i))
+                    out_banks[i, half] = psum.tile([P, 2, HALF], F32, name="bank%d" % (N_PAIRS * half + i))
                 for u in range(2):
                     n0 = (2 * i + u) * P
                     nc.tensor.matmul_mx(
-                        out=acc[i, half][:, u, :],
+                        out=out_banks[i, half][:, u, :],
                         lhsT=w4[:, b, 2 * n0 : 2 * (n0 + P)].bitcast(FP4X4),
                         lhsT_scale=w4_s[:, b, n0 : n0 + P],
-                        rhs=eq[b][:, cols].bitcast(FP8X4),
-                        rhs_scale=eq_s[b][:, cols],
+                        rhs=e_q[b][:, cols].bitcast(FP8X4),
+                        rhs_scale=e_s[b][:, cols],
                         start=(b == 0 and u == 0),
-                        stop=(b == HP - 1 and u == 1),
+                        stop=(b == R_PASSES - 1 and u == 1),
                     )
 
         def finish(half):
             cols = slice(half * HALF, (half + 1) * HALF)
-            for i in range(len(res)):
-                nc.vector.tensor_tensor(res[i][:, :, cols], acc[i, half][:], res[i][:, :, cols], ALU.add)
+            for i in range(N_PAIRS):
+                nc.vector.tensor_tensor(result[i][:, :, cols], out_banks[i, half][:], result[i][:, :, cols], ALU.add)
                 rows = out[2 * P * i : 2 * P * (i + 1), cols]
-                nc.sync.dma_start(out=rows.rearrange("(u p) m -> p u m", p=P), in_=res[i][:, :, cols])
+                nc.sync.dma_start(out=rows.rearrange("(u p) m -> p u m", p=P), in_=result[i][:, :, cols])
 
         nc.vector.tensor_copy(v_s[:], tab_s[:].indirect(idx[:]))
-        for a in range(KP):
-            gather_tab(a)
-            last = a == KP - 1
-            cast_w1(0, a, 80 if last else 0)
-            quant_w1(0, a, 4 if last else 1)
-            first_product(0, a)
+        for a in range(K_PASSES):
+            nc.vector.tensor_copy(v[a][:], tab[a][:].bitcast(U32).indirect(idx[:]))
+            if a < K_PASSES - 1:
+                quantise_w1(0, a, nc.scalar.copy, 1)
+            else:
+                quantise_w1(0, a, nc.vector.tensor_copy, PACK)
+            for t in range(PACK):
+                first_product(0, t, a)
 
-        evacuate(0, 0)
-        look(0, 0, 0, M)
-        cast_w1(1, 0, 0)
+        for a in range(K_PASSES):
+            quantise_w1(1, a, nc.scalar.copy, 1 if a < K_PASSES - 1 else 2)
         for t in range(PACK):
-            if t + 1 < PACK:
-                evacuate(0, t + 1)
-                look(0, t + 1, 0, M)
-            pick(0, t, 0, M)
-            if t > 0:
-                product(0, t - 1, 0, M)
-            if t == 1:
-                quant_w1(1, 0, 1)
-                first_product(1, 0)
-                cast_w1(1, 1, 0)
-        cast_w1(1, 2, 0)
-        quant_w1(1, 1, 1)
-        first_product(1, 1)
-        product(0, PACK - 1, 0, M)
-        quant_w1(1, 2, 4)
-        first_product(1, 2)
-        group_e(0, 0, M)
+            evacuate(0, t)
+        for t in range(PACK):
+            for a in range(K_PASSES):
+                first_product(1, t, a)
+        for t in range(PACK):
+            evacuate(1, t)
 
-        evacuate(1, 0)
-        look(1, 0, 0, HALF)
         for t in range(PACK):
-            if t + 1 < PACK:
-                evacuate(1, t + 1)
-                look(1, t + 1, 0, HALF)
-            pick(1, t, 0, HALF)
-            if t > 0:
-                product(1, t - 1, 0, HALF)
-            if t == 1:
-                quant_e(0, 0, M)
-        second_product(0, 0)
-        second_product(0, 1)
-        for t in range(PACK):
-            look(1, t, HALF, HALF)
-        pick(1, 0, HALF, HALF)
-        product(1, PACK - 1, 0, HALF)
-        group_e(1, 0, HALF)
-        for t in range(PACK):
-            if t + 1 < PACK:
-                pick(1, t + 1, HALF, HALF)
-            product(1, t, HALF, HALF)
-        group_e(1, HALF, HALF)
-        quant_e(1, 0, HALF)
-        second_product(1, 0)
-        finish(0)
-        quant_e(1, HALF, HALF)
-        second_product(1, 1)
-        finish(1)
+            make_e(0, t, 0, M)
+        for half in range(2):
+            for t in range(PACK):
+                make_e(1, t, half * HALF, HALF)
+            for b in range(R_PASSES):
+                quantise_e(b, half)
+                second_product(b, half)
+        for half in range(2):
+            finish(half)

@@ -156,13 +156,20 @@ def tile_list_ward_alarm_board_kernel(
             cols = slice(lo, lo + n)
             entries = slice(lo // PER_COLUMN, (lo + n) // PER_COLUMN)
             look = looked[b, t][:, cols]
+            e = e_rows[b][:, t, cols]
+            row_gain = gains[:, b, t : t + 1]
+            pick = h[b, t][:].indirect(p2[:, entries])
             nc.scalar.activation(out=look, in_=h[b, t][:].indirect(p1[:, entries]), func=ACT.Exp, bias=neg_top[b, t][:])
-            nc.scalar.activation(out=look, in_=look, func=ACT.Copy, scale=gains[:, b, t : t + 1])
-            nc.vector.tensor_tensor(e_rows[b][:, t, cols], h[b, t][:].indirect(p2[:, entries]), look, ALU.mult)
+            if b == 0:
+                nc.vector.tensor_copy(e, pick)
+                nc.vector.scalar_tensor_tensor(out=e, in0=e, scalar=row_gain, in1=look, op0=ALU.mult, op1=ALU.mult)
+            else:
+                nc.scalar.activation(out=look, in_=look, func=ACT.Copy, scale=row_gain)
+                nc.vector.tensor_tensor(e, pick, look, ALU.mult)
 
-        def quantise_e(b, half):
+        def quantise_e(b, half, copy):
             cols = slice(half * HALF, (half + 1) * HALF)
-            nc.scalar.copy(
+            copy(
                 out=e_words[b][:, cols, :].rearrange("p (c i) t -> p c t i", i=4),
                 in_=e_rows[b][:, :, cols].rearrange("p t (c i) -> p c t i", i=4),
             )
@@ -208,8 +215,9 @@ def tile_list_ward_alarm_board_kernel(
             for t in range(PACK):
                 first_product(0, t, a)
 
-        for a in range(K_PASSES):
-            quantise_w1(1, a, nc.scalar.copy, 1 if a < K_PASSES - 1 else 2)
+        for a in range(K_PASSES - 1):
+            quantise_w1(1, a, nc.scalar.copy, 1)
+        quantise_w1(1, K_PASSES - 1, nc.vector.tensor_copy, 2)
         for t in range(PACK):
             evacuate(0, t)
         for t in range(PACK):
@@ -224,7 +232,8 @@ def tile_list_ward_alarm_board_kernel(
             for t in range(PACK):
                 make_e(1, t, half * HALF, HALF)
             for b in range(R_PASSES):
-                quantise_e(b, half)
+                last = b == R_PASSES - 1 and half == 1
+                quantise_e(b, half, nc.vector.tensor_copy if last else nc.scalar.copy)
                 second_product(b, half)
         for half in range(2):
             finish(half)

from contextlib import ExitStack

import concourse.mybir as mybir

K, H, N, T, S, M = 1536, 1024, 768, 4096, 1024, 512
FLOPS = 2 * K * H * S + 2 * H * N * M

F32 = mybir.dt.float32
BF16 = mybir.dt.bfloat16
I32 = mybir.dt.int32
U32 = mybir.dt.uint32
U16 = mybir.dt.uint16
U8 = mybir.dt.uint8
FP8X4 = mybir.dt.float8_e4m3fn_x4
FP4X4 = mybir.dt.float4_e2m1fn_x4
ALU = mybir.AluOpType
ACT = mybir.ActivationFunctionType

P = 128
PACK = 4
PASS = P * PACK
K_PASSES = K // PASS
R_PASSES = H // PASS
QUADRANTS = 4
BANK = 512
HALF = M // 2
N_PAIRS = N // (2 * P)
PER_COLUMN = 16


def tile_list_ward_alarm_board_kernel(
    tc, tab_words, tab_scales, offs, pos1, pos2, w1, gain, w4_words, w4_scales, last_round, out
):
    nc = tc.nc
    w1_chunks = [(b, a) for b in range(R_PASSES) for a in range(K_PASSES)]
    row_sets = [(b, t) for b in range(R_PASSES) for t in range(PACK)]

    with ExitStack() as ctx:
        lists = ctx.enter_context(tc.tile_pool(name="lists", bufs=1))
        keep = ctx.enter_context(tc.tile_pool(name="keep", bufs=1))
        stage = ctx.enter_context(tc.tile_pool(name="stage", bufs=K_PASSES))
        psum = ctx.enter_context(tc.psum_pool(name="psum", bufs=1))

        idx = lists.tile([P, S // PER_COLUMN], U16, name="idx")
        p1 = lists.tile([P, M // PER_COLUMN], U16, name="p1")
        p2 = lists.tile([P, M // PER_COLUMN], U16, name="p2")

        tab = [keep.tile([P, T], I32, name="tab%d" % a, align_bytes=64) for a in range(K_PASSES)]
        tab_s = keep.tile([P, T], U8, name="tab_s", align_bytes=64)
        v = [keep.tile([P, S], U32, name="v%d" % a, align_bytes=64) for a in range(K_PASSES)]
        v_s = keep.tile([P, S], U8, name="v_s", align_bytes=64)
        w1_raw = {c: keep.tile([P, PACK, PASS], F32, name="w1_raw%d%d" % c) for c in w1_chunks}
        w1_q = {c: keep.tile([P, PASS], U32, name="w1_q%d%d" % c, align_bytes=64) for c in w1_chunks}
        w1_s = {c: keep.tile([P, PASS], U8, name="w1_s%d%d" % c, align_bytes=64) for c in w1_chunks}
        gains = keep.tile([P, R_PASSES, PACK], F32, name="gains")
        w4 = keep.tile([P, R_PASSES, 2 * N], U8, name="w4", align_bytes=64)
        w4_s = keep.tile([P, R_PASSES, N], U8, name="w4_s", align_bytes=64)
        result = [keep.tile([P, 2, M], F32, name="result%d" % i) for i in range(N_PAIRS)]
        h = {r: keep.tile([P, S], F32, name="h%d%d" % r) for r in row_sets}
        bank_tops = {r: keep.tile([P, S // BANK], F32, name="bank_tops%d%d" % r) for r in row_sets}
        neg_top = {r: keep.tile([P, 1], F32, name="neg_top%d%d" % r) for r in row_sets}
        looked = {r: keep.tile([P, M], F32, name="looked%d%d" % r) for r in row_sets}
        e_rows = [keep.tile([P, PACK, M], F32, name="e_rows%d" % b) for b in range(R_PASSES)]
        e_words = [keep.tile([P, M, PACK], BF16, name="e_words%d" % b, align_bytes=64) for b in range(R_PASSES)]
        e_q = [keep.tile([P, M], U32, name="e_q%d" % b, align_bytes=64) for b in range(R_PASSES)]
        e_s = [keep.tile([P, M], U8, name="e_s%d" % b, align_bytes=64) for b in range(R_PASSES)]

        def load_table(a):
            nc.sync.dma_start(out=tab[a][:], in_=tab_words[a].rearrange("p n i -> p (n i)").bitcast(I32))

        def load_w1(b, a):
            rows = w1[a * PASS : (a + 1) * PASS, b * PASS : (b + 1) * PASS]
            nc.sync.dma_start(out=w1_raw[b, a][:], in_=rows.rearrange("(p j) c -> p j c", j=PACK))

        nc.vector.memset(tab_s[:].bitcast(I32), 0)
        nc.vector.memset(w4_s[:].bitcast(I32), 0)
        load_table(0)
        for q in range(QUADRANTS):
            nc.sync.dma_start(
                out=tab_s[32 * q : 32 * q + 4 * K_PASSES, :].bitcast(I32),
                in_=tab_scales[:, 4 * q : 4 * q + 4, :].bitcast(I32),
            )
        nc.sync.dma_start(idx[:], offs)
        load_w1(0, 0)
        for a in range(1, K_PASSES):
            load_table(a)
            load_w1(0, a)
        nc.sync.dma_start(out=gains[:], in_=gain.rearrange("(b p t) -> p b t", b=R_PASSES, t=PACK))
        nc.sync.dma_start(p1[:], pos1)
        nc.sync.dma_start(p2[:], pos2)
        for a in range(K_PASSES):
            load_w1(1, a)
        nc.sync.dma_start(out=w4[:].bitcast(I32), in_=w4_words.rearrange("b p c -> p b c").bitcast(I32))
        for q in range(QUADRANTS):
            nc.sync.dma_start(
                out=w4_s[32 * q : 32 * q + 4, :, :].bitcast(I32),
                in_=w4_scales[:, 4 * q : 4 * q + 4, :].rearrange("b r n -> r b n").bitcast(I32),
            )
        for i in range(N_PAIRS):
            rows = last_round[2 * P * i : 2 * P * (i + 1), :]
            nc.sync.dma_start(out=result[i][:], in_=rows.rearrange("(u p) m -> p u m", p=P))

        def quantise_w1(b, a, first_copy, pieces):
            rounded = stage.tile([P, PACK, P, PACK], BF16, name="rounded", align_bytes=64)
            src = w1_raw[b, a][:].rearrange("p j (m u s) -> p u m j s", u=2, s=2)
            dst = rounded[:].rearrange("p (u s) m j -> p u m j s", u=2)
            first_copy(out=dst[:, 0], in_=src[:, 0])
            nc.scalar.copy(out=dst[:, 1], in_=src[:, 1])
            flat = rounded[:].rearrange("p t m j -> p (t m j)")
            width = PASS // pieces
            for lo in range(0, PASS, width):
                nc.vector.quantize_mx(
                    out=w1_q[b, a][:, lo : lo + width].bitcast(FP8X4),
                    scales=w1_s[b, a][:, lo : lo + width],
                    in_=flat[:, lo * PACK : (lo + width) * PACK],
                )

        h_banks = {}

        def first_product(b, t, a):
            for c in range(S // BANK):
                if a == 0:
                    h_banks[b, t, c] = psum.tile([P, BANK], F32, name="bank%d" % (t * (S // BANK) + c))
                cols = slice(c * BANK, (c + 1) * BANK)
                nc.tensor.matmul_mx(
                    out=h_banks[b, t, c][:],
                    lhsT=w1_q[b, a][:, t * P : (t + 1) * P].bitcast(FP8X4),
                    lhsT_scale=w1_s[b, a][:, t * P : (t + 1) * P],
                    rhs=v[a][:, cols].bitcast(FP8X4),
                    rhs_scale=v_s[4 * a : P, cols],
                    start=(a == 0),
                    stop=(a == K_PASSES - 1),
                )

        def evacuate(b, t):
            for c in range(S // BANK):
                nc.vector.tensor_scalar(
                    out=h[b, t][:, c * BANK : (c + 1) * BANK],
                    in0=h_banks[b, t, c][:],
                    scalar1=1.0,
                    scalar2=None,
                    op0=ALU.mult,
                    op1=ALU.max,
                    accum_out=bank_tops[b, t][:, c : c + 1],
                )
            nc.gpsimd.tensor_scalar(
                out=neg_top[b, t][:],
                in0=bank_tops[b, t][:, 0:1],
                scalar1=bank_tops[b, t][:, 1:2],
                scalar2=-1.0,
                op0=ALU.max,
                op1=ALU.mult,
            )

        def make_e(b, t, lo, n):
            cols = slice(lo, lo + n)
            entries = slice(lo // PER_COLUMN, (lo + n) // PER_COLUMN)
            look = looked[b, t][:, cols]
            e = e_rows[b][:, t, cols]
            row_gain = gains[:, b, t : t + 1]
            pick = h[b, t][:].indirect(p2[:, entries])
            nc.scalar.activation(out=look, in_=h[b, t][:].indirect(p1[:, entries]), func=ACT.Exp, bias=neg_top[b, t][:])
            if b == 0:
                nc.vector.tensor_copy(e, pick)
                nc.vector.scalar_tensor_tensor(out=e, in0=e, scalar=row_gain, in1=look, op0=ALU.mult, op1=ALU.mult)
            else:
                nc.scalar.activation(out=look, in_=look, func=ACT.Copy, scale=row_gain)
                nc.vector.tensor_tensor(e, pick, look, ALU.mult)

        def quantise_e(b, half, copy):
            cols = slice(half * HALF, (half + 1) * HALF)
            copy(
                out=e_words[b][:, cols, :].rearrange("p (c i) t -> p c t i", i=4),
                in_=e_rows[b][:, :, cols].rearrange("p t (c i) -> p c t i", i=4),
            )
            nc.vector.quantize_mx(
                out=e_q[b][:, cols].bitcast(FP8X4),
                scales=e_s[b][:, cols],
                in_=e_words[b][:, cols, :].rearrange("p m t -> p (m t)"),
            )

        out_banks = {}

        def second_product(b, half):
            cols = slice(half * HALF, (half + 1) * HALF)
            for i in range(N_PAIRS):
                if b == 0:
                    out_banks[i, half] = psum.tile([P, 2, HALF], F32, name="bank%d" % (N_PAIRS * half + i))
                for u in range(2):
                    n0 = (2 * i + u) * P
                    nc.tensor.matmul_mx(
                        out=out_banks[i, half][:, u, :],
                        lhsT=w4[:, b, 2 * n0 : 2 * (n0 + P)].bitcast(FP4X4),
                        lhsT_scale=w4_s[:, b, n0 : n0 + P],
                        rhs=e_q[b][:, cols].bitcast(FP8X4),
                        rhs_scale=e_s[b][:, cols],
                        start=(b == 0 and u == 0),
                        stop=(b == R_PASSES - 1 and u == 1),
                    )

        def finish(half):
            cols = slice(half * HALF, (half + 1) * HALF)
            for i in range(N_PAIRS):
                nc.vector.tensor_tensor(result[i][:, :, cols], out_banks[i, half][:], result[i][:, :, cols], ALU.add)
                rows = out[2 * P * i : 2 * P * (i + 1), cols]
                nc.sync.dma_start(out=rows.rearrange("(u p) m -> p u m", p=P), in_=result[i][:, :, cols])

        nc.vector.tensor_copy(v_s[:], tab_s[:].indirect(idx[:]))
        for a in range(K_PASSES):
            nc.vector.tensor_copy(v[a][:], tab[a][:].bitcast(U32).indirect(idx[:]))
            if a < K_PASSES - 1:
                quantise_w1(0, a, nc.scalar.copy, 1)
            else:
                quantise_w1(0, a, nc.vector.tensor_copy, PACK)
            for t in range(PACK):
                first_product(0, t, a)

        for a in range(K_PASSES - 1):
            quantise_w1(1, a, nc.scalar.copy, 1)
        quantise_w1(1, K_PASSES - 1, nc.vector.tensor_copy, 2)
        for t in range(PACK):
            evacuate(0, t)
        for t in range(PACK):
            for a in range(K_PASSES):
                first_product(1, t, a)
        for t in range(PACK):
            evacuate(1, t)

        for t in range(PACK):
            make_e(0, t, 0, M)
        for half in range(2):
            for t in range(PACK):
                make_e(1, t, half * HALF, HALF)
            for b in range(R_PASSES):
                last = b == R_PASSES - 1 and half == 1
                quantise_e(b, half, nc.vector.tensor_copy if last else nc.scalar.copy)
                second_product(b, half)
        for half in range(2):
            finish(half)
